import numpy as np
import ml_dtypes


def mxq(x, axis, fmt="e4m3"):
    dtype, down = {"e4m3": (ml_dtypes.float8_e4m3fn, 7), "e5m2": (ml_dtypes.float8_e5m2, 14)}[fmt]
    v = np.moveaxis(np.asarray(x, np.float32).astype(ml_dtypes.bfloat16).astype(np.float64), axis, -1)
    blocks = v.reshape(v.shape[:-1] + (-1, 32))
    amax = np.abs(blocks).max(-1, keepdims=True)
    byte = np.maximum(np.where(amax > 0, np.frexp(amax)[1] - 1 + 127, 0) - down, 1)
    scale = np.exp2(byte - 127.0)
    codes = (blocks / scale).astype(np.float32).astype(dtype).astype(np.float64)
    return np.moveaxis((codes * scale).reshape(v.shape), -1, axis)


WIDE = False


def mx_kscale(k):
    if not WIDE:
        return np.ones(k)
    levels = np.array([10, -10, 5, -5, 0])
    if k % 512:
        return np.exp2(np.random.permutation(np.resize(levels, k // 32))).repeat(32)
    a = np.empty((k // 512, 16))
    for p in range(k // 512):
        a[p, :8] = np.random.permutation(np.resize(levels, 8))
        for g in range(8):
            far = levels[np.abs(levels - a[p, g]) >= 10]
            a[p, g + 8] = far[np.random.randint(len(far))]
    return np.exp2(a.ravel()).repeat(32)


def f64(x):
    return np.asarray(x).astype(np.float64)


def striped(idx):
    return np.tile(np.asarray(idx).reshape(-1, 16).T, (8, 1)).astype(np.uint16)


def unstriped(offs):
    return offs[:16].T.reshape(-1).astype(np.int64)


B, N, T, D, DV, NQ = 1, 512, 1024, 512, 256, 128
NEW = 128


def setup_inputs():
    n = np.random.standard_normal
    idx = np.random.permutation(T)[:B * N]
    s = mx_kscale(D)[:, None]
    u = np.ones(T)
    u[idx] = mx_kscale(B * N)
    r = np.random.uniform(0.5, 2.0, T)
    k = n((D, T)) / s
    v = n((DV, T)) / (u * r)
    new = np.random.permutation(idx.reshape(B, N)[:, -NEW // B:].reshape(-1))
    return {
        "qT": (n((B, D, NQ)) * s * (0.90 / np.sqrt(D))).astype(np.float32),
        "kT": np.where(np.isin(np.arange(T), new)[None, :], n((D, T)), k).astype(np.float32),
        "vT": np.where(np.isin(np.arange(T), new)[None, :], n((DV, T)), v).astype(np.float32),
        "new_kT": k[:, new].astype(np.float32),
        "new_vT": v[:, new].astype(np.float32),
        "vs": np.tile(u * r, (128, 1)).astype(np.float32),
        "offs": striped(idx),
        "slots": striped(new),
    }


def reference(qT, kT, vT, new_kT, new_vT, vs, offs, slots):
    idx = unstriped(offs)
    k = f64(kT)
    k[:, unstriped(slots)] = f64(new_kT)
    v = f64(vT)
    v[:, unstriped(slots)] = f64(new_vT)
    pick = lambda x: x[:, idx].reshape(x.shape[0], B, N).transpose(1, 0, 2)
    q = f64(qT)
    score = mxq(q, 1, "e4m3").transpose(0, 2, 1) @ mxq(pick(k), 1, "e4m3")
    m = score.max(-1, keepdims=True)
    p = np.exp(score - m)
    total = p.sum(-1, keepdims=True)
    w = p * pick(f64(vs))[:, :1, :]
    y = mxq(w, 2, "e4m3") @ mxq(pick(v).transpose(0, 2, 1), 1, "e4m3")
    y = y / total
    return y

@@ -1,0 +1,146 @@
+from contextlib import ExitStack
+
+import concourse.mybir as mybir
+from concourse.masks import make_identity
+
+P = 128
+T, N, DV, NQ, NEW = 1024, 512, 256, 128, 128
+FLOPS = 2 * NQ * N * (512 + DV)
+
+F32 = mybir.dt.float32
+BF16 = mybir.dt.bfloat16
+U32 = mybir.dt.uint32
+U16 = mybir.dt.uint16
+U8 = mybir.dt.uint8
+FP8X4 = mybir.dt.float8_e4m3fn_x4
+COPY = mybir.ActivationFunctionType.Copy
+EXP = mybir.ActivationFunctionType.Exp
+MULT = mybir.AluOpType.mult
+MAX = mybir.AluOpType.max
+AX = mybir.AxisListType.X
+
+
+def tile_attend_kv_append128_kernel(tc, qT, kT, vT, new_kT, new_vT, vs, offs, slots, out):
+    nc = tc.nc
+    with ExitStack() as ctx:
+        pool = ctx.enter_context(tc.tile_pool(name="keep", bufs=1))
+        psum = ctx.enter_context(tc.psum_pool(name="psum", bufs=1))
+
+        offs_sb = pool.tile([P, N // 16], U16, name="offs_sb")
+        slots_sb = pool.tile([P, NEW // 16], U16, name="slots_sb")
+
+        k_view = kT.rearrange("(p t) n -> p t n", t=4)
+        nk_view = new_kT.rearrange("(p t) n -> p t n", t=4)
+        v_view = vT.rearrange("(u p) n -> p u n", p=P)
+        nv_view = new_vT.rearrange("(u p) n -> p u n", p=P)
+        q_view = qT[0].rearrange("(p t) q -> p t q", t=4)
+
+        kp = [pool.tile([P, T], F32, name=f"kp{t}") for t in range(4)]
+        vp = [pool.tile([P, T], F32, name=f"vp{u}") for u in range(2)]
+        nk_hi = pool.tile([P, 2, NEW], F32, name="nk_hi")
+        nk_lo = pool.tile([P, 2, NEW], F32, name="nk_lo")
+        nv = pool.tile([P, 2, NEW], F32, name="nv")
+        qf = pool.tile([P, 4, NQ], F32, name="qf")
+        vs_sb = pool.tile([P, T], F32, name="vs_sb")
+
+        nc.sync.dma_start(slots_sb[:], slots)
+        nc.sync.dma_start(nk_hi[:], nk_view[:, 2:4, :])
+        nc.sync.dma_start(kp[2][:], k_view[:, 2, :])
+        nc.sync.dma_start(kp[3][:], k_view[:, 3, :])
+        nc.sync.dma_start(offs_sb[:], offs)
+        nc.sync.dma_start(nk_lo[:], nk_view[:, 0:2, :])
+        nc.sync.dma_start(kp[0][:], k_view[:, 0, :])
+        nc.sync.dma_start(kp[1][:], k_view[:, 1, :])
+        nc.sync.dma_start(qf[:], q_view)
+        nc.sync.dma_start(nv[:], nv_view)
+        nc.sync.dma_start(vp[0][:], v_view[:, 0, :])
+        nc.sync.dma_start(vp[1][:], v_view[:, 1, :])
+        nc.sync.dma_start(vs_sb[:], vs)
+
+        warm = pool.tile([P, 1], F32, name="warm")
+        nc.gpsimd.memset(warm[:], 0.0)
+        warm_out = pool.tile([P, 1], F32, name="warm_out")
+        nc.scalar.activation(warm_out[:], warm[:], EXP)
+
+        ident_f = pool.tile([P, P], F32, name="ident_f")
+        make_identity(nc, ident_f[:])
+        ident_b = pool.tile([P, P], BF16, name="ident_b")
+        make_identity(nc, ident_b[:])
+
+        kb2 = pool.tile([P, T], BF16, name="kb2")
+        kb3 = pool.tile([P, T], BF16, name="kb3")
+        kg = pool.tile([P, N, 4], BF16, name="kg", align_bytes=64)
+
+        def scatter(window, values):
+            nc.vector.tensor_copy(window[:].indirect(slots_sb[:]), values)
+
+        scatter(kp[2], nk_hi[:, 0, :])
+        nc.scalar.activation(kb2[:], kp[2][:], COPY)
+        scatter(kp[3], nk_hi[:, 1, :])
+        nc.scalar.activation(kg[:, :, 2], kb2[:].indirect(offs_sb[:]), COPY)
+        scatter(kp[0], nk_lo[:, 0, :])
+        nc.scalar.activation(kb3[:], kp[3][:], COPY)
+        nc.vector.tensor_copy(kg[:, :, 0], kp[0][:].indirect(offs_sb[:]))
+        nc.scalar.activation(kg[:, :, 3], kb3[:].indirect(offs_sb[:]), COPY)
+        scatter(kp[1], nk_lo[:, 1, :])
+        nc.vector.tensor_copy(kg[:, :, 1], kp[1][:].indirect(offs_sb[:]))
+
+        qg = pool.tile([P, NQ, 4], BF16, name="qg", align_bytes=64)
+        nc.scalar.activation(qg[:], qf[:].rearrange("p t q -> p q t"), COPY)
+        qc = pool.tile([P, NQ], U32, name="qc", align_bytes=64)
+        qs = pool.tile([P, NQ], U8, name="qs", align_bytes=64)
+        nc.vector.quantize_mx(out=qc[:].bitcast(FP8X4), scales=qs[:], in_=qg[:].rearrange("p q t -> p (q t)"))
+
+        kc = pool.tile([P, N], U32, name="kc", align_bytes=64)
+        ks = pool.tile([P, N], U8, name="ks", align_bytes=64)
+        nc.vector.quantize_mx(out=kc[:].bitcast(FP8X4), scales=ks[:], in_=kg[:].rearrange("p n t -> p (n t)"))
+
+        score = psum.tile([P, N], F32, name="score")
+        nc.tensor.matmul_mx(out=score[:], lhsT=qc[:].bitcast(FP8X4), lhsT_scale=qs[:], rhs=kc[:].bitcast(FP8X4), rhs_scale=ks[:], start=True, stop=True)
+
+        scatter(vp[0], nv[:, 0, :])
+
+        neg_m = pool.tile([P, 1], F32, name="neg_m")
+        nc.vector.tensor_reduce(out=neg_m[:], in_=score[:], axis=AX, op=MAX, negate=True)
+        p_sb = pool.tile([P, N], F32, name="p_sb")
+        total = pool.tile([P, 1], F32, name="total")
+        nc.scalar.activation(p_sb[:], score[:], EXP, bias=neg_m[:], accum_out=total[:])
+
+        scatter(vp[1], nv[:, 1, :])
+
+        vb0 = pool.tile([P, T], BF16, name="vb0")
+        vg = [pool.tile([P, 4, P], BF16, name=f"vg{u}", align_bytes=64) for u in range(2)]
+        nc.scalar.activation(vb0[:], vp[0][:], COPY)
+        nc.scalar.activation(vg[0][:].rearrange("p t s -> p s t"), vb0[:].indirect(offs_sb[:]), COPY)
+
+        w_sb = pool.tile([P, N], F32, name="w_sb")
+        nc.vector.tensor_tensor(w_sb[:], vs_sb[:].indirect(offs_sb[:]), p_sb[:], MULT)
+        rtot = pool.tile([P, 1], F32, name="rtot")
+
+        wt = psum.tile([P, 4, NQ], F32, name="wt")
+        for t in range(4):
+            nc.tensor.transpose(wt[:, t, :], w_sb[:, t:N:4], ident_f[:])
+        wg = pool.tile([P, NQ, 4], BF16, name="wg", align_bytes=64)
+        nc.scalar.activation(wg[:], wt[:].rearrange("s t q -> s q t"), COPY)
+
+        nc.vector.tensor_copy(vg[1][:].rearrange("p t s -> p s t"), vp[1][:].indirect(offs_sb[:]))
+        nc.vector.reciprocal(rtot[:], total[:])
+
+        wc = pool.tile([P, NQ], U32, name="wc", align_bytes=64)
+        ws = pool.tile([P, NQ], U8, name="ws", align_bytes=64)
+        nc.vector.quantize_mx(out=wc[:].bitcast(FP8X4), scales=ws[:], in_=wg[:].rearrange("s q t -> s (q t)"))
+
+        for u in range(2):
+            vt = psum.tile([P, 4, P], BF16, name=f"vt{u}")
+            for t in range(4):
+                nc.tensor.transpose(vt[:, t, :], vg[u][:, t, :], ident_b[:])
+            vi = pool.tile([P, P, 4], BF16, name=f"vi{u}", align_bytes=64)
+            nc.scalar.copy(vi[:], vt[:].rearrange("s t e -> s e t"))
+            vc = pool.tile([P, P], U32, name=f"vc{u}", align_bytes=64)
+            vsc = pool.tile([P, P], U8, name=f"vsc{u}", align_bytes=64)
+            nc.vector.quantize_mx(out=vc[:].bitcast(FP8X4), scales=vsc[:], in_=vi[:].rearrange("s e t -> s (e t)"))
+            y = psum.tile([P, P], F32, name=f"y{u}")
+            nc.tensor.matmul_mx(out=y[:], lhsT=wc[:].bitcast(FP8X4), lhsT_scale=ws[:], rhs=vc[:].bitcast(FP8X4), rhs_scale=vsc[:], start=True, stop=True)
+            o_sb = pool.tile([P, P], F32, name=f"o_sb{u}")
+            nc.scalar.activation(o_sb[:], y[:], COPY, scale=rtot[:])
+            nc.sync.dma_start(out[0][:, u * P : (u + 1) * P], o_sb[:])

@@ -16,6 +16,7 @@ FP8X4 = mybir.dt.float8_e4m3fn_x4
 COPY = mybir.ActivationFunctionType.Copy
 EXP = mybir.ActivationFunctionType.Exp
 MULT = mybir.AluOpType.mult
+ADD = mybir.AluOpType.add
 MAX = mybir.AluOpType.max
 AX = mybir.AxisListType.X
 
@@ -28,119 +29,143 @@ def tile_attend_kv_append128_kernel(tc, qT, kT, vT, new_kT, new_vT, vs, offs, sl
 
         offs_sb = pool.tile([P, N // 16], U16, name="offs_sb")
         slots_sb = pool.tile([P, NEW // 16], U16, name="slots_sb")
-
         k_view = kT.rearrange("(p t) n -> p t n", t=4)
         nk_view = new_kT.rearrange("(p t) n -> p t n", t=4)
         v_view = vT.rearrange("(u p) n -> p u n", p=P)
         nv_view = new_vT.rearrange("(u p) n -> p u n", p=P)
         q_view = qT[0].rearrange("(p t) q -> p t q", t=4)
-
         kp = [pool.tile([P, T], F32, name=f"kp{t}") for t in range(4)]
         vp = [pool.tile([P, T], F32, name=f"vp{u}") for u in range(2)]
         nk_hi = pool.tile([P, 2, NEW], F32, name="nk_hi")
         nk_lo = pool.tile([P, 2, NEW], F32, name="nk_lo")
-        nv = pool.tile([P, 2, NEW], F32, name="nv")
+        nv_sb = pool.tile([P, 2, NEW], F32, name="nv_sb")
+        nk = [nk_lo[:, 0, :], nk_lo[:, 1, :], nk_hi[:, 0, :], nk_hi[:, 1, :]]
+        nv = [nv_sb[:, 0, :], nv_sb[:, 1, :]]
         qf = pool.tile([P, 4, NQ], F32, name="qf")
         vs_sb = pool.tile([P, T], F32, name="vs_sb")
-
-        nc.sync.dma_start(slots_sb[:], slots)
         nc.sync.dma_start(nk_hi[:], nk_view[:, 2:4, :])
-        nc.sync.dma_start(kp[2][:], k_view[:, 2, :])
+        nc.sync.dma_start(slots_sb[:], slots)
         nc.sync.dma_start(kp[3][:], k_view[:, 3, :])
+        nc.sync.dma_start(kp[2][:], k_view[:, 2, :])
         nc.sync.dma_start(offs_sb[:], offs)
-        nc.sync.dma_start(nk_lo[:], nk_view[:, 0:2, :])
-        nc.sync.dma_start(kp[0][:], k_view[:, 0, :])
         nc.sync.dma_start(kp[1][:], k_view[:, 1, :])
+        nc.sync.dma_start(nk_lo[:], nk_view[:, 0:2, :])
         nc.sync.dma_start(qf[:], q_view)
-        nc.sync.dma_start(nv[:], nv_view)
+        nc.sync.dma_start(nv_sb[:], nv_view)
+        nc.sync.dma_start(kp[0][:], k_view[:, 0, :])
         nc.sync.dma_start(vp[0][:], v_view[:, 0, :])
-        nc.sync.dma_start(vp[1][:], v_view[:, 1, :])
         nc.sync.dma_start(vs_sb[:], vs)
+        nc.sync.dma_start(vp[1][:], v_view[:, 1, :])
 
         warm = pool.tile([P, 1], F32, name="warm")
         nc.gpsimd.memset(warm[:], 0.0)
         warm_out = pool.tile([P, 1], F32, name="warm_out")
         nc.scalar.activation(warm_out[:], warm[:], EXP)
-
-        ident_f = pool.tile([P, P], F32, name="ident_f")
-        make_identity(nc, ident_f[:])
         ident_b = pool.tile([P, P], BF16, name="ident_b")
         make_identity(nc, ident_b[:])
+        ident_f = pool.tile([P, P], F32, name="ident_f")
+        make_identity(nc, ident_f[:])
 
-        kb2 = pool.tile([P, T], BF16, name="kb2")
-        kb3 = pool.tile([P, T], BF16, name="kb3")
+        kb = [pool.tile([P, T], BF16, name=f"kb{t}") for t in range(4)]
+        vb = [pool.tile([P, T], BF16, name=f"vb{u}") for u in range(2)]
+        gq = pool.tile([P, 4, 4, P], BF16, name="gq", align_bytes=64)
+        g_cols = gq[:].rearrange("p j t s -> p j (t s)")
+        vg = [pool.tile([P, 4, P], BF16, name=f"vg{u}", align_bytes=64) for u in range(2)]
+        vi = pool.tile([P, DV, 4], BF16, name="vi", align_bytes=64)
         kg = pool.tile([P, N, 4], BF16, name="kg", align_bytes=64)
+        qg = pool.tile([P, NQ, 4], BF16, name="qg", align_bytes=64)
+        wg = pool.tile([P, NQ, 4], BF16, name="wg", align_bytes=64)
+        vs_g = pool.tile([P, N], F32, name="vs_g")
+        vs_col = pool.tile([P, 4], F32, name="vs_col")
+        p_sb = pool.tile([P, 4, P], F32, name="p_sb")
+        neg_m = pool.tile([P, 1], F32, name="neg_m")
+        total = pool.tile([P, 1], F32, name="total")
+        rtot = pool.tile([P, 1], F32, name="rtot")
+        o_sb = [pool.tile([P, P], F32, name=f"o_sb{u}") for u in range(2)]
+        score = psum.tile([P, N], F32, name="score")
+        pt = psum.tile([P, 4, NQ], F32, name="pt")
+        vs_t = psum.tile([P, 4, P], F32, name="vs_t")
+        vt = [psum.tile([P, 4, P], BF16, name=f"vt{u}") for u in range(2)]
+        y = [psum.tile([P, P], F32, name=f"y{u}") for u in range(2)]
+
+        def mx_tiles(name, width):
+            codes = pool.tile([P, width], U32, name=name + "_codes", align_bytes=64)
+            scales = pool.tile([P, width], U8, name=name + "_scales", align_bytes=64)
+            return codes, scales
+
+        q_mx = mx_tiles("q", NQ)
+        k_mx = mx_tiles("k", N)
+        w_mx = mx_tiles("w", NQ)
+        v_mx = mx_tiles("v", DV)
 
         def scatter(window, values):
             nc.vector.tensor_copy(window[:].indirect(slots_sb[:]), values)
 
-        scatter(kp[2], nk_hi[:, 0, :])
-        nc.scalar.activation(kb2[:], kp[2][:], COPY)
-        scatter(kp[3], nk_hi[:, 1, :])
-        nc.scalar.activation(kg[:, :, 2], kb2[:].indirect(offs_sb[:]), COPY)
-        scatter(kp[0], nk_lo[:, 0, :])
-        nc.scalar.activation(kb3[:], kp[3][:], COPY)
-        nc.vector.tensor_copy(kg[:, :, 0], kp[0][:].indirect(offs_sb[:]))
-        nc.scalar.activation(kg[:, :, 3], kb3[:].indirect(offs_sb[:]), COPY)
-        scatter(kp[1], nk_lo[:, 1, :])
-        nc.vector.tensor_copy(kg[:, :, 1], kp[1][:].indirect(offs_sb[:]))
+        def quarters(dst):
+            return dst.rearrange("p t s -> p s t")
 
-        qg = pool.tile([P, NQ, 4], BF16, name="qg", align_bytes=64)
-        nc.scalar.activation(qg[:], qf[:].rearrange("p t q -> p q t"), COPY)
-        qc = pool.tile([P, NQ], U32, name="qc", align_bytes=64)
-        qs = pool.tile([P, NQ], U8, name="qs", align_bytes=64)
-        nc.vector.quantize_mx(out=qc[:].bitcast(FP8X4), scales=qs[:], in_=qg[:].rearrange("p q t -> p (q t)"))
+        def gather_scalar(dst, window):
+            nc.scalar.activation(dst, window[:].indirect(offs_sb[:]), COPY)
 
-        kc = pool.tile([P, N], U32, name="kc", align_bytes=64)
-        ks = pool.tile([P, N], U8, name="ks", align_bytes=64)
-        nc.vector.quantize_mx(out=kc[:].bitcast(FP8X4), scales=ks[:], in_=kg[:].rearrange("p n t -> p (n t)"))
+        def gather_vector(dst, window):
+            nc.vector.tensor_copy(dst, window[:].indirect(offs_sb[:]))
 
-        score = psum.tile([P, N], F32, name="score")
-        nc.tensor.matmul_mx(out=score[:], lhsT=qc[:].bitcast(FP8X4), lhsT_scale=qs[:], rhs=kc[:].bitcast(FP8X4), rhs_scale=ks[:], start=True, stop=True)
+        def scalar_copy(dst, rows):
+            nc.scalar.activation(dst, rows, COPY)
 
-        scatter(vp[0], nv[:, 0, :])
+        def lay_side_by_side(copy, dst, rows):
+            copy(dst.rearrange("p (c i) t -> p c t i", i=4), rows.rearrange("p t (c i) -> p c t i", i=4))
 
-        neg_m = pool.tile([P, 1], F32, name="neg_m")
-        nc.vector.tensor_reduce(out=neg_m[:], in_=score[:], axis=AX, op=MAX, negate=True)
-        p_sb = pool.tile([P, N], F32, name="p_sb")
-        total = pool.tile([P, 1], F32, name="total")
-        nc.scalar.activation(p_sb[:], score[:], EXP, bias=neg_m[:], accum_out=total[:])
+        def quantize(mx, grouped):
+            nc.vector.quantize_mx(out=mx[0][:].bitcast(FP8X4), scales=mx[1][:], in_=grouped.rearrange("p c t -> p (c t)"))
 
-        scatter(vp[1], nv[:, 1, :])
+        def multiply(bank, lhs, rhs, cols):
+            nc.tensor.matmul_mx(out=bank, lhsT=lhs[0][:].bitcast(FP8X4), lhsT_scale=lhs[1][:], rhs=rhs[0][:, cols].bitcast(FP8X4), rhs_scale=rhs[1][:, cols], start=True, stop=True)
 
-        vb0 = pool.tile([P, T], BF16, name="vb0")
-        vg = [pool.tile([P, 4, P], BF16, name=f"vg{u}", align_bytes=64) for u in range(2)]
-        nc.scalar.activation(vb0[:], vp[0][:], COPY)
-        nc.scalar.activation(vg[0][:].rearrange("p t s -> p s t"), vb0[:].indirect(offs_sb[:]), COPY)
-
-        w_sb = pool.tile([P, N], F32, name="w_sb")
-        nc.vector.tensor_tensor(w_sb[:], vs_sb[:].indirect(offs_sb[:]), p_sb[:], MULT)
-        rtot = pool.tile([P, 1], F32, name="rtot")
-
-        wt = psum.tile([P, 4, NQ], F32, name="wt")
-        for t in range(4):
-            nc.tensor.transpose(wt[:, t, :], w_sb[:, t:N:4], ident_f[:])
-        wg = pool.tile([P, NQ, 4], BF16, name="wg", align_bytes=64)
-        nc.scalar.activation(wg[:], wt[:].rearrange("s t q -> s q t"), COPY)
-
-        nc.vector.tensor_copy(vg[1][:].rearrange("p t s -> p s t"), vp[1][:].indirect(offs_sb[:]))
-        nc.vector.reciprocal(rtot[:], total[:])
-
-        wc = pool.tile([P, NQ], U32, name="wc", align_bytes=64)
-        ws = pool.tile([P, NQ], U8, name="ws", align_bytes=64)
-        nc.vector.quantize_mx(out=wc[:].bitcast(FP8X4), scales=ws[:], in_=wg[:].rearrange("s q t -> s (q t)"))
-
-        for u in range(2):
-            vt = psum.tile([P, 4, P], BF16, name=f"vt{u}")
+        def transpose_quarters(bank, src, ident):
             for t in range(4):
-                nc.tensor.transpose(vt[:, t, :], vg[u][:, t, :], ident_b[:])
-            vi = pool.tile([P, P, 4], BF16, name=f"vi{u}", align_bytes=64)
-            nc.scalar.copy(vi[:], vt[:].rearrange("s t e -> s e t"))
-            vc = pool.tile([P, P], U32, name=f"vc{u}", align_bytes=64)
-            vsc = pool.tile([P, P], U8, name=f"vsc{u}", align_bytes=64)
-            nc.vector.quantize_mx(out=vc[:].bitcast(FP8X4), scales=vsc[:], in_=vi[:].rearrange("s e t -> s (e t)"))
-            y = psum.tile([P, P], F32, name=f"y{u}")
-            nc.tensor.matmul_mx(out=y[:], lhsT=wc[:].bitcast(FP8X4), lhsT_scale=ws[:], rhs=vc[:].bitcast(FP8X4), rhs_scale=vsc[:], start=True, stop=True)
-            o_sb = pool.tile([P, P], F32, name=f"o_sb{u}")
-            nc.scalar.activation(o_sb[:], y[:], COPY, scale=rtot[:])
-            nc.sync.dma_start(out[0][:, u * P : (u + 1) * P], o_sb[:])
+                nc.tensor.transpose(bank[:, t, :], src[:, t, :], ident[:])
+
+        scatter(kp[2], nk[2])
+        scalar_copy(kb[2][:], kp[2][:])
+        scatter(kp[3], nk[3])
+        nc.vector.tensor_copy(kb[3][:], kp[3][:])
+        scatter(vp[1], nv[1])
+        nc.vector.tensor_copy(vs_g[:], vs_sb[:].indirect(offs_sb[:]))
+        scatter(kp[0], nk[0])
+        gather_vector(quarters(gq[:, 0]), kp[0])
+        gather_scalar(quarters(gq[:, 3]), kb[3])
+        scatter(vp[0], nv[0])
+        scalar_copy(vb[0][:], vp[0][:])
+        gather_scalar(quarters(vg[0][:]), vb[0])
+        transpose_quarters(vt[0], vg[0], ident_b)
+        nc.scalar.copy(vi[:, :P, :], vt[0][:].rearrange("s t e -> s e t"))
+        for t in range(4):
+            nc.tensor.transpose(vs_t[:, t, :], vs_g[:, t:N:4], ident_f[:])
+        scalar_copy(vs_col[:], vs_t[:, :, 0])
+        gather_vector(quarters(vg[1][:]), vp[1])
+        transpose_quarters(vt[1], vg[1], ident_b)
+        scatter(kp[1], nk[1])
+        nc.vector.tensor_copy(kb[1][:], kp[1][:])
+        nc.gpsimd.tensor_scalar(qg[:], qf[:].rearrange("p t q -> p q t"), 1.0, 0.0, MULT, ADD)
+        quantize(q_mx, qg[:])
+        gather_scalar(quarters(gq[:, 2]), kb[2])
+        gather_scalar(quarters(gq[:, 1]), kb[1])
+        lay_side_by_side(nc.vector.tensor_copy, kg[:, :256, :], g_cols[:, :, :256])
+        lay_side_by_side(nc.scalar.copy, kg[:, 256:, :], g_cols[:, :, 256:])
+        quantize(k_mx, kg[:])
+        multiply(score[:], q_mx, k_mx, slice(0, N))
+        nc.vector.tensor_reduce(out=neg_m[:], in_=score[:], axis=AX, op=MAX, negate=True)
+        nc.scalar.activation(p_sb[:], score[:].rearrange("q (t s) -> q t s", t=4), EXP, bias=neg_m[:], accum_out=total[:])
+        nc.vector.reciprocal(rtot[:], total[:])
+        transpose_quarters(pt, p_sb, ident_f)
+        nc.vector.tensor_tensor(wg[:], pt[:].rearrange("s t q -> s q t"), vs_col[:].unsqueeze(1).to_broadcast([P, NQ, 4]), MULT)
+        quantize(w_mx, wg[:])
+        nc.vector.tensor_copy(vi[:, P:, :], vt[1][:].rearrange("s t e -> s e t"))
+        quantize(v_mx, vi[:])
+        multiply(y[1][:], w_mx, v_mx, slice(P, DV))
+        nc.vector.tensor_scalar(o_sb[1][:], y[1][:], rtot[:], None, MULT)
+        nc.sync.dma_start(out[0][:, 1 * P : 2 * P], o_sb[1][:])
+        multiply(y[0][:], w_mx, v_mx, slice(0, P))
+        nc.scalar.activation(o_sb[0][:], y[0][:], COPY, scale=rtot[:])
+        nc.sync.dma_start(out[0][:, 0 * P : 1 * P], o_sb[0][:])

@@ -43,13 +43,13 @@ def tile_attend_kv_append128_kernel(tc, qT, kT, vT, new_kT, new_vT, vs, offs, sl
         nv = [nv_sb[:, 0, :], nv_sb[:, 1, :]]
         qf = pool.tile([P, 4, NQ], F32, name="qf")
         vs_sb = pool.tile([P, T], F32, name="vs_sb")
-        nc.sync.dma_start(nk_hi[:], nk_view[:, 2:4, :])
-        nc.sync.dma_start(slots_sb[:], slots)
-        nc.sync.dma_start(kp[3][:], k_view[:, 3, :])
         nc.sync.dma_start(kp[2][:], k_view[:, 2, :])
+        nc.sync.dma_start(slots_sb[:], slots)
+        nc.sync.dma_start(nk_hi[:], nk_view[:, 2:4, :])
+        nc.sync.dma_start(kp[3][:], k_view[:, 3, :])
+        nc.sync.dma_start(nk_lo[:], nk_view[:, 0:2, :])
         nc.sync.dma_start(offs_sb[:], offs)
         nc.sync.dma_start(kp[1][:], k_view[:, 1, :])
-        nc.sync.dma_start(nk_lo[:], nk_view[:, 0:2, :])
         nc.sync.dma_start(qf[:], q_view)
         nc.sync.dma_start(nv_sb[:], nv_view)
         nc.sync.dma_start(kp[0][:], k_view[:, 0, :])
@@ -71,7 +71,7 @@ def tile_attend_kv_append128_kernel(tc, qT, kT, vT, new_kT, new_vT, vs, offs, sl
         gq = pool.tile([P, 4, 4, P], BF16, name="gq", align_bytes=64)
         g_cols = gq[:].rearrange("p j t s -> p j (t s)")
         vg = [pool.tile([P, 4, P], BF16, name=f"vg{u}", align_bytes=64) for u in range(2)]
-        vi = pool.tile([P, DV, 4], BF16, name="vi", align_bytes=64)
+        vi = [pool.tile([P, P, 4], BF16, name=f"vi{u}", align_bytes=64) for u in range(2)]
         kg = pool.tile([P, N, 4], BF16, name="kg", align_bytes=64)
         qg = pool.tile([P, NQ, 4], BF16, name="qg", align_bytes=64)
         wg = pool.tile([P, NQ, 4], BF16, name="wg", align_bytes=64)
@@ -96,7 +96,7 @@ def tile_attend_kv_append128_kernel(tc, qT, kT, vT, new_kT, new_vT, vs, offs, sl
         q_mx = mx_tiles("q", NQ)
         k_mx = mx_tiles("k", N)
         w_mx = mx_tiles("w", NQ)
-        v_mx = mx_tiles("v", DV)
+        v_mx = [mx_tiles("v0", P), mx_tiles("v1", P)]
 
         def scatter(window, values):
             nc.vector.tensor_copy(window[:].indirect(slots_sb[:]), values)
@@ -119,53 +119,54 @@ def tile_attend_kv_append128_kernel(tc, qT, kT, vT, new_kT, new_vT, vs, offs, sl
         def quantize(mx, grouped):
             nc.vector.quantize_mx(out=mx[0][:].bitcast(FP8X4), scales=mx[1][:], in_=grouped.rearrange("p c t -> p (c t)"))
 
-        def multiply(bank, lhs, rhs, cols):
-            nc.tensor.matmul_mx(out=bank, lhsT=lhs[0][:].bitcast(FP8X4), lhsT_scale=lhs[1][:], rhs=rhs[0][:, cols].bitcast(FP8X4), rhs_scale=rhs[1][:, cols], start=True, stop=True)
+        def multiply(bank, lhs, rhs):
+            nc.tensor.matmul_mx(out=bank, lhsT=lhs[0][:].bitcast(FP8X4), lhsT_scale=lhs[1][:], rhs=rhs[0][:].bitcast(FP8X4), rhs_scale=rhs[1][:], start=True, stop=True)
 
         def transpose_quarters(bank, src, ident):
             for t in range(4):
                 nc.tensor.transpose(bank[:, t, :], src[:, t, :], ident[:])
 
         scatter(kp[2], nk[2])
+        nc.gpsimd.tensor_scalar(qg[:], qf[:].rearrange("p t q -> p q t"), 1.0, 0.0, MULT, ADD)
+        scatter(kp[1], nk[1])
+        nc.vector.tensor_copy(kb[1][:], kp[1][:])
         scalar_copy(kb[2][:], kp[2][:])
+        gather_scalar(quarters(gq[:, 2]), kb[2])
+        gather_scalar(quarters(gq[:, 1]), kb[1])
+        quantize(q_mx, qg[:])
         scatter(kp[3], nk[3])
         nc.vector.tensor_copy(kb[3][:], kp[3][:])
-        scatter(vp[1], nv[1])
-        nc.vector.tensor_copy(vs_g[:], vs_sb[:].indirect(offs_sb[:]))
-        scatter(kp[0], nk[0])
-        gather_vector(quarters(gq[:, 0]), kp[0])
         gather_scalar(quarters(gq[:, 3]), kb[3])
         scatter(vp[0], nv[0])
         scalar_copy(vb[0][:], vp[0][:])
+        scatter(vp[1], nv[1])
         gather_scalar(quarters(vg[0][:]), vb[0])
+        scatter(kp[0], nk[0])
+        gather_vector(quarters(gq[:, 0]), kp[0])
+        lay_side_by_side(nc.vector.tensor_copy, kg[:, :256, :], g_cols[:, :, :256])
         transpose_quarters(vt[0], vg[0], ident_b)
-        nc.scalar.copy(vi[:, :P, :], vt[0][:].rearrange("s t e -> s e t"))
+        nc.scalar.copy(vi[0][:], vt[0][:].rearrange("s t e -> s e t"))
+        gather_vector(quarters(vg[1][:]), vp[1])
+        transpose_quarters(vt[1], vg[1], ident_b)
+        nc.scalar.copy(vi[1][:], vt[1][:].rearrange("s t e -> s e t"))
+        nc.vector.tensor_copy(vs_g[:], vs_sb[:].indirect(offs_sb[:]))
         for t in range(4):
             nc.tensor.transpose(vs_t[:, t, :], vs_g[:, t:N:4], ident_f[:])
         scalar_copy(vs_col[:], vs_t[:, :, 0])
-        gather_vector(quarters(vg[1][:]), vp[1])
-        transpose_quarters(vt[1], vg[1], ident_b)
-        scatter(kp[1], nk[1])
-        nc.vector.tensor_copy(kb[1][:], kp[1][:])
-        nc.gpsimd.tensor_scalar(qg[:], qf[:].rearrange("p t q -> p q t"), 1.0, 0.0, MULT, ADD)
-        quantize(q_mx, qg[:])
-        gather_scalar(quarters(gq[:, 2]), kb[2])
-        gather_scalar(quarters(gq[:, 1]), kb[1])
-        lay_side_by_side(nc.vector.tensor_copy, kg[:, :256, :], g_cols[:, :, :256])
         lay_side_by_side(nc.scalar.copy, kg[:, 256:, :], g_cols[:, :, 256:])
         quantize(k_mx, kg[:])
-        multiply(score[:], q_mx, k_mx, slice(0, N))
+        multiply(score[:], q_mx, k_mx)
         nc.vector.tensor_reduce(out=neg_m[:], in_=score[:], axis=AX, op=MAX, negate=True)
         nc.scalar.activation(p_sb[:], score[:].rearrange("q (t s) -> q t s", t=4), EXP, bias=neg_m[:], accum_out=total[:])
-        nc.vector.reciprocal(rtot[:], total[:])
         transpose_quarters(pt, p_sb, ident_f)
         nc.vector.tensor_tensor(wg[:], pt[:].rearrange("s t q -> s q t"), vs_col[:].unsqueeze(1).to_broadcast([P, NQ, 4]), MULT)
+        nc.vector.reciprocal(rtot[:], total[:])
         quantize(w_mx, wg[:])
-        nc.vector.tensor_copy(vi[:, P:, :], vt[1][:].rearrange("s t e -> s e t"))
-        quantize(v_mx, vi[:])
-        multiply(y[1][:], w_mx, v_mx, slice(P, DV))
+        quantize(v_mx[1], vi[1][:])
+        multiply(y[1][:], w_mx, v_mx[1])
         nc.vector.tensor_scalar(o_sb[1][:], y[1][:], rtot[:], None, MULT)
         nc.sync.dma_start(out[0][:, 1 * P : 2 * P], o_sb[1][:])
-        multiply(y[0][:], w_mx, v_mx, slice(0, P))
+        quantize(v_mx[0], vi[0][:])
+        multiply(y[0][:], w_mx, v_mx[0])
         nc.scalar.activation(o_sb[0][:], y[0][:], COPY, scale=rtot[:])
         nc.sync.dma_start(out[0][:, 0 * P : 1 * P], o_sb[0][:])

from contextlib import ExitStack

import concourse.mybir as mybir
from concourse.masks import make_identity

P = 128
T, N, DV, NQ, NEW = 1024, 512, 256, 128, 128
FLOPS = 2 * NQ * N * (512 + DV)

F32 = mybir.dt.float32
BF16 = mybir.dt.bfloat16
U32 = mybir.dt.uint32
U16 = mybir.dt.uint16
U8 = mybir.dt.uint8
FP8X4 = mybir.dt.float8_e4m3fn_x4
COPY = mybir.ActivationFunctionType.Copy
EXP = mybir.ActivationFunctionType.Exp
MULT = mybir.AluOpType.mult
ADD = mybir.AluOpType.add
MAX = mybir.AluOpType.max
AX = mybir.AxisListType.X


def tile_attend_kv_append128_kernel(tc, qT, kT, vT, new_kT, new_vT, vs, offs, slots, out):
    nc = tc.nc
    with ExitStack() as ctx:
        pool = ctx.enter_context(tc.tile_pool(name="keep", bufs=1))
        psum = ctx.enter_context(tc.psum_pool(name="psum", bufs=1))

        offs_sb = pool.tile([P, N // 16], U16, name="offs_sb")
        slots_sb = pool.tile([P, NEW // 16], U16, name="slots_sb")
        k_view = kT.rearrange("(p t) n -> p t n", t=4)
        nk_view = new_kT.rearrange("(p t) n -> p t n", t=4)
        v_view = vT.rearrange("(u p) n -> p u n", p=P)
        nv_view = new_vT.rearrange("(u p) n -> p u n", p=P)
        q_view = qT[0].rearrange("(p t) q -> p t q", t=4)
        kp = [pool.tile([P, T], F32, name=f"kp{t}") for t in range(4)]
        vp = [pool.tile([P, T], F32, name=f"vp{u}") for u in range(2)]
        nk_hi = pool.tile([P, 2, NEW], F32, name="nk_hi")
        nk_lo = pool.tile([P, 2, NEW], F32, name="nk_lo")
        nv_sb = pool.tile([P, 2, NEW], F32, name="nv_sb")
        nk = [nk_lo[:, 0, :], nk_lo[:, 1, :], nk_hi[:, 0, :], nk_hi[:, 1, :]]
        nv = [nv_sb[:, 0, :], nv_sb[:, 1, :]]
        qf = pool.tile([P, 4, NQ], F32, name="qf")
        vs_sb = pool.tile([P, T], F32, name="vs_sb")
        nc.sync.dma_start(kp[2][:], k_view[:, 2, :])
        nc.sync.dma_start(slots_sb[:], slots)
        nc.sync.dma_start(nk_hi[:], nk_view[:, 2:4, :])
        nc.sync.dma_start(kp[3][:], k_view[:, 3, :])
        nc.sync.dma_start(nk_lo[:], nk_view[:, 0:2, :])
        nc.sync.dma_start(offs_sb[:], offs)
        nc.sync.dma_start(kp[1][:], k_view[:, 1, :])
        nc.sync.dma_start(qf[:], q_view)
        nc.sync.dma_start(nv_sb[:], nv_view)
        nc.sync.dma_start(kp[0][:], k_view[:, 0, :])
        nc.sync.dma_start(vp[0][:], v_view[:, 0, :])
        nc.sync.dma_start(vs_sb[:], vs)
        nc.sync.dma_start(vp[1][:], v_view[:, 1, :])

        warm = pool.tile([P, 1], F32, name="warm")
        nc.gpsimd.memset(warm[:], 0.0)
        warm_out = pool.tile([P, 1], F32, name="warm_out")
        nc.scalar.activation(warm_out[:], warm[:], EXP)
        ident_b = pool.tile([P, P], BF16, name="ident_b")
        make_identity(nc, ident_b[:])
        ident_f = pool.tile([P, P], F32, name="ident_f")
        make_identity(nc, ident_f[:])

        kb = [pool.tile([P, T], BF16, name=f"kb{t}") for t in range(4)]
        vb = [pool.tile([P, T], BF16, name=f"vb{u}") for u in range(2)]
        gq = pool.tile([P, 4, 4, P], BF16, name="gq", align_bytes=64)
        g_cols = gq[:].rearrange("p j t s -> p j (t s)")
        vg = [pool.tile([P, 4, P], BF16, name=f"vg{u}", align_bytes=64) for u in range(2)]
        vi = [pool.tile([P, P, 4], BF16, name=f"vi{u}", align_bytes=64) for u in range(2)]
        kg = pool.tile([P, N, 4], BF16, name="kg", align_bytes=64)
        qg = pool.tile([P, NQ, 4], BF16, name="qg", align_bytes=64)
        wg = pool.tile([P, NQ, 4], BF16, name="wg", align_bytes=64)
        vs_g = pool.tile([P, N], F32, name="vs_g")
        vs_col = pool.tile([P, 4], F32, name="vs_col")
        p_sb = pool.tile([P, 4, P], F32, name="p_sb")
        neg_m = pool.tile([P, 1], F32, name="neg_m")
        total = pool.tile([P, 1], F32, name="total")
        rtot = pool.tile([P, 1], F32, name="rtot")
        o_sb = [pool.tile([P, P], F32, name=f"o_sb{u}") for u in range(2)]
        score = psum.tile([P, N], F32, name="score")
        pt = psum.tile([P, 4, NQ], F32, name="pt")
        vs_t = psum.tile([P, 4, P], F32, name="vs_t")
        vt = [psum.tile([P, 4, P], BF16, name=f"vt{u}") for u in range(2)]
        y = [psum.tile([P, P], F32, name=f"y{u}") for u in range(2)]

        def mx_tiles(name, width):
            codes = pool.tile([P, width], U32, name=name + "_codes", align_bytes=64)
            scales = pool.tile([P, width], U8, name=name + "_scales", align_bytes=64)
            return codes, scales

        q_mx = mx_tiles("q", NQ)
        k_mx = mx_tiles("k", N)
        w_mx = mx_tiles("w", NQ)
        v_mx = [mx_tiles("v0", P), mx_tiles("v1", P)]

        def scatter(window, values):
            nc.vector.tensor_copy(window[:].indirect(slots_sb[:]), values)

        def quarters(dst):
            return dst.rearrange("p t s -> p s t")

        def gather_scalar(dst, window):
            nc.scalar.activation(dst, window[:].indirect(offs_sb[:]), COPY)

        def gather_vector(dst, window):
            nc.vector.tensor_copy(dst, window[:].indirect(offs_sb[:]))

        def scalar_copy(dst, rows):
            nc.scalar.activation(dst, rows, COPY)

        def lay_side_by_side(copy, dst, rows):
            copy(dst.rearrange("p (c i) t -> p c t i", i=4), rows.rearrange("p t (c i) -> p c t i", i=4))

        def quantize(mx, grouped):
            nc.vector.quantize_mx(out=mx[0][:].bitcast(FP8X4), scales=mx[1][:], in_=grouped.rearrange("p c t -> p (c t)"))

        def multiply(bank, lhs, rhs):
            nc.tensor.matmul_mx(out=bank, lhsT=lhs[0][:].bitcast(FP8X4), lhsT_scale=lhs[1][:], rhs=rhs[0][:].bitcast(FP8X4), rhs_scale=rhs[1][:], start=True, stop=True)

        def transpose_quarters(bank, src, ident):
            for t in range(4):
                nc.tensor.transpose(bank[:, t, :], src[:, t, :], ident[:])

        scatter(kp[2], nk[2])
        nc.gpsimd.tensor_scalar(qg[:], qf[:].rearrange("p t q -> p q t"), 1.0, 0.0, MULT, ADD)
        scatter(kp[1], nk[1])
        nc.vector.tensor_copy(kb[1][:], kp[1][:])
        scalar_copy(kb[2][:], kp[2][:])
        gather_scalar(quarters(gq[:, 2]), kb[2])
        gather_scalar(quarters(gq[:, 1]), kb[1])
        quantize(q_mx, qg[:])
        scatter(kp[3], nk[3])
        nc.vector.tensor_copy(kb[3][:], kp[3][:])
        gather_scalar(quarters(gq[:, 3]), kb[3])
        scatter(vp[0], nv[0])
        scalar_copy(vb[0][:], vp[0][:])
        scatter(vp[1], nv[1])
        gather_scalar(quarters(vg[0][:]), vb[0])
        scatter(kp[0], nk[0])
        gather_vector(quarters(gq[:, 0]), kp[0])
        lay_side_by_side(nc.vector.tensor_copy, kg[:, :256, :], g_cols[:, :, :256])
        transpose_quarters(vt[0], vg[0], ident_b)
        nc.scalar.copy(vi[0][:], vt[0][:].rearrange("s t e -> s e t"))
        gather_vector(quarters(vg[1][:]), vp[1])
        transpose_quarters(vt[1], vg[1], ident_b)
        nc.scalar.copy(vi[1][:], vt[1][:].rearrange("s t e -> s e t"))
        nc.vector.tensor_copy(vs_g[:], vs_sb[:].indirect(offs_sb[:]))
        for t in range(4):
            nc.tensor.transpose(vs_t[:, t, :], vs_g[:, t:N:4], ident_f[:])
        scalar_copy(vs_col[:], vs_t[:, :, 0])
        lay_side_by_side(nc.scalar.copy, kg[:, 256:, :], g_cols[:, :, 256:])
        quantize(k_mx, kg[:])
        multiply(score[:], q_mx, k_mx)
        nc.vector.tensor_reduce(out=neg_m[:], in_=score[:], axis=AX, op=MAX, negate=True)
        nc.scalar.activation(p_sb[:], score[:].rearrange("q (t s) -> q t s", t=4), EXP, bias=neg_m[:], accum_out=total[:])
        transpose_quarters(pt, p_sb, ident_f)
        nc.vector.tensor_tensor(wg[:], pt[:].rearrange("s t q -> s q t"), vs_col[:].unsqueeze(1).to_broadcast([P, NQ, 4]), MULT)
        nc.vector.reciprocal(rtot[:], total[:])
        quantize(w_mx, wg[:])
        quantize(v_mx[1], vi[1][:])
        multiply(y[1][:], w_mx, v_mx[1])
        nc.vector.tensor_scalar(o_sb[1][:], y[1][:], rtot[:], None, MULT)
        nc.sync.dma_start(out[0][:, 1 * P : 2 * P], o_sb[1][:])
        quantize(v_mx[0], vi[0][:])
        multiply(y[0][:], w_mx, v_mx[0])
        nc.scalar.activation(o_sb[0][:], y[0][:], COPY, scale=rtot[:])
        nc.sync.dma_start(out[0][:, 0 * P : 1 * P], o_sb[0][:])
